import numpy as np, ml_dtypes
CORES = [40,64,80,88,96,104,120,144]
N = 8
import mx_ref
NC, GR, GC, T = 512, 2, 4, 4
TA, TB = T // GC, T // GR
BF = ml_dtypes.bfloat16
def setup_inputs(rng):
    def f(*shape):
        return mx_ref.flush((rng.standard_normal(shape, dtype=np.float32) * np.exp2(rng.integers(-2, 3, shape[:-1] + (1,)))).astype(BF))
    return {"a": f(N, 128, TA * 512), "b": f(N, 128, TB * 4 * NC)}
def reference(a, b):
    A = lambda i, s: mx_ref.quantize(a[i * GC + s // TA][:, 512 * (s % TA):512 * (s % TA) + 512])
    B = lambda s, j: mx_ref.quantize(b[(s // TB) * GC + j][:, 4 * NC * (s % TB):4 * NC * (s % TB) + 4 * NC])
    y = np.zeros((N, 128, NC), np.float32)
    for r in range(N):
        for s in range(T):
            p = mx_ref.matmul(A(r // GC, s), B(s, r % GC))
            y[r] = p if s == 0 else y[r] + p
    return {"y": y}

@@ -1,0 +1,166 @@
+from concourse.bass import DstId, RemoteDMATransfer
+from concourse.mybir import dt
+
+GR, GC = 2, 4
+NC = 512
+AC = 128
+WIDTHS = [256, 256]
+K = len(WIDTHS)
+START = [sum(WIDTHS[:k]) for k in range(K)]
+HOSTS = 2
+
+SCRATCH = {
+    "abf": ("sbuf", [128, 4 * AC], "bfloat16"),
+    "bbf": ("sbuf", [128, 2 * 4 * NC], "bfloat16"),
+    "aq": ("sbuf", [128, GC * AC], "float8_e4m3fn_x4"),
+    "asc": ("sbuf", [128, GC * AC], "uint8"),
+    "bq": ("sbuf", [128, 2 * NC], "float8_e4m3fn_x4"),
+    "bsc": ("sbuf", [128, 2 * NC], "uint8"),
+    "rq": ("sbuf", [128, 2 * NC], "float8_e4m3fn_x4"),
+    "rsc": ("sbuf", [128, 2 * NC], "uint8"),
+    "ps": ("psum", [128, 512 * K], "float32"),
+    "ysb": ("sbuf", [128, NC], "float32"),
+}
+CODES = ("aq", "bq", "rq")
+NCALLS = 2 + 2 * K
+SEMAPHORES = (["lda", "qa", "aarr", "sent", "stored"]
+              + ["ldb%d" % k for k in range(K)] + ["qb%d" % k for k in range(K)] + ["rem%d" % k for k in range(K)]
+              + ["mm%d" % k for k in range(K)] + ["ev%d" % k for k in range(K)] + ["in%d" % c for c in range(NCALLS)])
+
+
+def engines(mask):
+    return [e for e in range(mask.bit_length()) if (mask >> e) & 1]
+
+
+def as_mask(es):
+    return sum(1 << e for e in es)
+
+
+def view(T, name, lo, hi):
+    ap = T[name][:, lo:hi]
+    return ap.bitcast(dt.uint8) if name in CODES else ap
+
+
+def block(k, m=0):
+    return 2 * START[k] + m * WIDTHS[k]
+
+
+def plan(rk, T, topo):
+    r = T.rank_of(rk)
+    i, j = r // GC, r % GC
+    partner = T.cores[(GR - 1 - i) * GC + j]
+    row = [T.cores[i * GC + c] for c in range(GC) if c != j]
+    chip = [c for c in range(HOSTS * topo.CORES_PER_HOST)
+            if c != rk and topo.host(c) == topo.host(rk) and topo.chip(c) == topo.chip(rk)]
+    porters = [c for c in chip if topo.may_write(c, partner)]
+    near = [c for c in porters if topo.die(c) == topo.die(rk)]
+    far = [c for c in porters if topo.die(c) != topo.die(rk)]
+    barred = [d for d in row if not topo.may_write(rk, d)]
+    free = [d for d in row if topo.may_write(rk, d)]
+    lo, hi = AC * j, AC * j + AC
+    calls = [
+        ("qa", [("asc", "asc", lo, hi, "all",
+                 [(near[0], barred[0], "aarr"), (far[0], barred[1], "aarr"), (near[1], free[0], "aarr")])]),
+        ("qa", [("aq", "aq", lo, hi, "all",
+                 [(near[0], barred[0], "aarr"), (far[0], barred[1], "aarr"), (far[1], free[0], "aarr")])]),
+    ]
+    for k in range(K):
+        w = WIDTHS[k]
+        calls.append(("qb%d" % k, [
+            ("bq", "rq", block(k, 0), block(k, 0) + w, "even", [(near[k % 2], partner, "rem%d" % k)]),
+            ("bq", "rq", block(k, 1), block(k, 1) + w, "odd", [(far[k % 2], partner, "rem%d" % k)])]))
+        calls.append(("qb%d" % k, [
+            ("bsc", "rsc", block(k), block(k) + 2 * w, "all", [(near[(k + 1) % 2], partner, "rem%d" % k)])]))
+    return calls
+
+
+def share(mask, which):
+    es = engines(mask)
+    return es if which == "all" else es[0::2] if which == "even" else es[1::2]
+
+
+def porter_program(g, core, rk, T, topo):
+    sent = 0
+    for c, (_, transfers) in enumerate(plan(rk, T, topo)):
+        for (_, land, lo, hi, which, hops) in transfers:
+            for (porter, dest, sem) in hops:
+                if porter != core:
+                    continue
+                g.wait_ge(T.sem["in%d" % c], len(share(topo.mask(rk, core), which)))
+                rid, pid = topo.addr(dest, core)
+                mask = topo.mask(core, dest)
+                g.remote_dma(view(T, land, lo, hi), view(T, land, lo, hi), T.sem[sem], T.sem.sent, pid, rid, mask)
+                sent += len(engines(mask))
+    if sent:
+        g.wait_ge(T.sem.sent, sent)
+
+
+def rank_program(g, core, T, topo):
+    rank = T.rank_of(core)
+    if rank is None:
+        for rk in T.cores:
+            if topo.host(rk) == topo.host(core) and topo.chip(rk) == topo.chip(core):
+                porter_program(g, core, rk, T, topo)
+        return
+    i, j = rank // GC, rank % GC
+
+    expect = {}
+    for rk in T.cores:
+        for (_, transfers) in plan(rk, T, topo):
+            for (_, _, _, _, _, hops) in transfers:
+                for (porter, dest, sem) in hops:
+                    if dest == core:
+                        expect[sem] = expect.get(sem, 0) + len(engines(topo.mask(porter, dest)))
+
+    g.sync.dma_start(T.abf[0:64, :], T.a[0:64, :]).then_inc(T.sem.lda, 16)
+    g.scalar.dma_start(T.abf[64:128, :], T.a[64:128, :]).then_inc(T.sem.lda, 16)
+    for k in range(K):
+        for m, q in ((0, g.sync), (1, g.scalar)):
+            q.dma_start(T.bbf[:, 4 * block(k, m):4 * (block(k, m) + WIDTHS[k])],
+                        T.b[:, 4 * (NC * m + START[k]):4 * (NC * m + START[k] + WIDTHS[k])]).then_inc(T.sem["ldb%d" % k], 16)
+
+    g.vector.wait_ge(T.sem.lda, 32)
+    g.vector.quantize_mx(T.aq[:, AC * j:AC * j + AC], T.asc[:, AC * j:AC * j + AC], T.abf[:]).then_inc(T.sem.qa, 1)
+    for k in range(K):
+        lo, hi = block(k), block(k) + 2 * WIDTHS[k]
+        g.vector.wait_ge(T.sem["ldb%d" % k], 32)
+        g.vector.quantize_mx(T.bq[:, lo:hi], T.bsc[:, lo:hi], T.bbf[:, 4 * lo:4 * hi]).then_inc(T.sem["qb%d" % k], 1)
+
+    sent = 0
+    for c, (ready, transfers) in enumerate(plan(core, T, topo)):
+        g.wait_ge(T.sem[ready], 1)
+        ts = []
+        for (src, land, lo, hi, which, hops) in transfers:
+            es = share(topo.mask(core, hops[0][0]), which)
+            ids = [topo.addr(porter, core) for (porter, _, _) in hops]
+            ts.append(RemoteDMATransfer(dst_ids=[DstId(rid=rid, pnc=pid) for (rid, pid) in ids],
+                                        dma_engine_mask=as_mask(es), remote_sem=T.sem["in%d" % c],
+                                        srcs=[view(T, src, lo, hi)], dsts=[view(T, land, lo, hi) for _ in hops]))
+            sent += len(es)
+        g.remote_dma_fused(ts, local_sem=T.sem.sent)
+
+    def products(k, q, sc, row, start, stop):
+        w = WIDTHS[k]
+        for m in range(2):
+            s = 2 * row + m
+            g.tensor.matmul_mx(T.ps[:, 512 * k:512 * k + w], T.aq[:, AC * s:AC * s + AC], T.asc[:, AC * s:AC * s + AC],
+                               q[:, block(k, m):block(k, m) + w], sc[:, block(k, m):block(k, m) + w],
+                               start and m == 0, stop and m == 1).then_inc(T.sem["mm%d" % k], 1)
+
+    g.tensor.wait_ge(T.sem.qa, 1)
+    g.tensor.wait_ge(T.sem.aarr, expect["aarr"])
+    for k in range(K):
+        g.tensor.wait_ge(T.sem["qb%d" % k], 1)
+        products(k, T.bq, T.bsc, i, True, False)
+    for k in range(K):
+        g.tensor.wait_ge(T.sem["rem%d" % k], expect["rem%d" % k])
+        products(k, T.rq, T.rsc, GR - 1 - i, False, True)
+
+    for k in range(K):
+        lo, hi = START[k], START[k] + WIDTHS[k]
+        g.vector.wait_ge(T.sem["mm%d" % k], 2 * GR)
+        g.vector.tensor_copy(T.ysb[:, lo:hi], T.ps[:, 512 * k:512 * k + WIDTHS[k]]).then_inc(T.sem["ev%d" % k], 1)
+        g.sync.wait_ge(T.sem["ev%d" % k], 1)
+        g.sync.dma_start(T.y[:, lo:hi], T.ysb[:, lo:hi]).then_inc(T.sem.stored, 16)
+    g.sync.wait_ge(T.sem.stored, 16 * K)
+    g.wait_ge(T.sem.sent, sent)

@@ -4,7 +4,7 @@ from concourse.mybir import dt
 GR, GC = 2, 4
 NC = 512
 AC = 128
-WIDTHS = [256, 256]
+WIDTHS = [128, 128, 128, 128]
 K = len(WIDTHS)
 START = [sum(WIDTHS[:k]) for k in range(K)]
 HOSTS = 2
@@ -22,8 +22,8 @@ SCRATCH = {
     "ysb": ("sbuf", [128, NC], "float32"),
 }
 CODES = ("aq", "bq", "rq")
-NCALLS = 2 + 2 * K
-SEMAPHORES = (["lda", "qa", "aarr", "sent", "stored"]
+NCALLS = 4 + 2 * K
+SEMAPHORES = (["lda", "qa", "sent", "stored"] + ["a%d" % s for s in range(GC)]
               + ["ldb%d" % k for k in range(K)] + ["qb%d" % k for k in range(K)] + ["rem%d" % k for k in range(K)]
               + ["mm%d" % k for k in range(K)] + ["ev%d" % k for k in range(K)] + ["in%d" % c for c in range(NCALLS)])
 
@@ -49,20 +49,22 @@ def plan(rk, T, topo):
     r = T.rank_of(rk)
     i, j = r // GC, r % GC
     partner = T.cores[(GR - 1 - i) * GC + j]
-    row = [T.cores[i * GC + c] for c in range(GC) if c != j]
+    on = [T.cores[i * GC + (j + o) % GC] for o in range(1, GC)]
     chip = [c for c in range(HOSTS * topo.CORES_PER_HOST)
             if c != rk and topo.host(c) == topo.host(rk) and topo.chip(c) == topo.chip(rk)]
-    porters = [c for c in chip if topo.may_write(c, partner)]
+    porters = [c for c in chip if all(topo.may_write(c, d) for d in [partner] + on)]
     near = [c for c in porters if topo.die(c) == topo.die(rk)]
     far = [c for c in porters if topo.die(c) != topo.die(rk)]
-    barred = [d for d in row if not topo.may_write(rk, d)]
-    free = [d for d in row if topo.may_write(rk, d)]
-    lo, hi = AC * j, AC * j + AC
+    barred = [d for d in on if not topo.may_write(rk, d)]
+    free = [d for d in on if topo.may_write(rk, d)]
+    if j % 2:
+        barred = barred[::-1]
+    lo, hi, sem = AC * j, AC * j + AC, "a%d" % j
     calls = [
-        ("qa", [("asc", "asc", lo, hi, "all",
-                 [(near[0], barred[0], "aarr"), (far[0], barred[1], "aarr"), (near[1], free[0], "aarr")])]),
-        ("qa", [("aq", "aq", lo, hi, "all",
-                 [(near[0], barred[0], "aarr"), (far[0], barred[1], "aarr"), (far[1], free[0], "aarr")])]),
+        ("qa", [("asc", "asc", lo, hi, "all", [(far[0], barred[0], sem), (near[0], barred[1], sem)])]),
+        ("qa", [("aq", "aq", lo, hi, "all", [(near[1], barred[0], sem), (far[1], barred[1], sem)])]),
+        ("qa", [("aq", "aq", lo, hi, "all", [(None, free[0], sem)])]),
+        ("qa", [("asc", "asc", lo, hi, "all", [(None, free[0], sem)])]),
     ]
     for k in range(K):
         w = WIDTHS[k]
@@ -70,8 +72,12 @@ def plan(rk, T, topo):
             ("bq", "rq", block(k, 0), block(k, 0) + w, "even", [(near[k % 2], partner, "rem%d" % k)]),
             ("bq", "rq", block(k, 1), block(k, 1) + w, "odd", [(far[k % 2], partner, "rem%d" % k)])]))
         calls.append(("qb%d" % k, [
-            ("bsc", "rsc", block(k), block(k) + 2 * w, "all", [(near[(k + 1) % 2], partner, "rem%d" % k)])]))
+            ("bsc", "rsc", block(k), block(k) + 2 * w, "all", [((near, far)[k % 2][(k + 1) % 2], partner, "rem%d" % k)])]))
     return calls
+
+
+def first_seen(xs):
+    return [x for n, x in enumerate(xs) if x not in xs[:n]]
 
 
 def share(mask, which):
@@ -107,10 +113,11 @@ def rank_program(g, core, T, topo):
     expect = {}
     for rk in T.cores:
         for (_, transfers) in plan(rk, T, topo):
-            for (_, _, _, _, _, hops) in transfers:
+            for (_, _, _, _, which, hops) in transfers:
                 for (porter, dest, sem) in hops:
                     if dest == core:
-                        expect[sem] = expect.get(sem, 0) + len(engines(topo.mask(porter, dest)))
+                        n = len(share(topo.mask(rk, dest), which)) if porter is None else len(engines(topo.mask(porter, dest)))
+                        expect[sem] = expect.get(sem, 0) + n
 
     g.sync.dma_start(T.abf[0:64, :], T.a[0:64, :]).then_inc(T.sem.lda, 16)
     g.scalar.dma_start(T.abf[64:128, :], T.a[64:128, :]).then_inc(T.sem.lda, 16)
@@ -131,30 +138,44 @@ def rank_program(g, core, T, topo):
         g.wait_ge(T.sem[ready], 1)
         ts = []
         for (src, land, lo, hi, which, hops) in transfers:
-            es = share(topo.mask(core, hops[0][0]), which)
-            ids = [topo.addr(porter, core) for (porter, _, _) in hops]
+            if hops[0][0] is None:
+                targets, landed = [hops[0][1]], T.sem[hops[0][2]]
+            else:
+                targets, landed = first_seen([h[0] for h in hops]), T.sem["in%d" % c]
+            es = share(topo.mask(core, targets[0]), which)
+            ids = [topo.addr(d, core) for d in targets]
             ts.append(RemoteDMATransfer(dst_ids=[DstId(rid=rid, pnc=pid) for (rid, pid) in ids],
-                                        dma_engine_mask=as_mask(es), remote_sem=T.sem["in%d" % c],
-                                        srcs=[view(T, src, lo, hi)], dsts=[view(T, land, lo, hi) for _ in hops]))
+                                        dma_engine_mask=as_mask(es), remote_sem=landed,
+                                        srcs=[view(T, src, lo, hi)], dsts=[view(T, land, lo, hi) for _ in ids]))
             sent += len(es)
         g.remote_dma_fused(ts, local_sem=T.sem.sent)
 
-    def products(k, q, sc, row, start, stop):
-        w = WIDTHS[k]
-        for m in range(2):
-            s = 2 * row + m
-            g.tensor.matmul_mx(T.ps[:, 512 * k:512 * k + w], T.aq[:, AC * s:AC * s + AC], T.asc[:, AC * s:AC * s + AC],
-                               q[:, block(k, m):block(k, m) + w], sc[:, block(k, m):block(k, m) + w],
-                               start and m == 0, stop and m == 1).then_inc(T.sem["mm%d" % k], 1)
+    def late(s):
+        return 0 if s == j else 1 if topo.may_write(T.cores[i * GC + s], core) else 2
 
-    g.tensor.wait_ge(T.sem.qa, 1)
-    g.tensor.wait_ge(T.sem.aarr, expect["aarr"])
-    for k in range(K):
-        g.tensor.wait_ge(T.sem["qb%d" % k], 1)
-        products(k, T.bq, T.bsc, i, True, False)
+    def stationary(s):
+        if s == j:
+            g.tensor.wait_ge(T.sem.qa, 1)
+        else:
+            g.tensor.wait_ge(T.sem["a%d" % s], expect["a%d" % s])
+
+    def product(k, s, q, sc, start, stop):
+        w, m = WIDTHS[k], s % 2
+        g.tensor.matmul_mx(T.ps[:, 512 * k:512 * k + w], T.aq[:, AC * s:AC * s + AC], T.asc[:, AC * s:AC * s + AC],
+                           q[:, block(k, m):block(k, m) + w], sc[:, block(k, m):block(k, m) + w],
+                           start, stop).then_inc(T.sem["mm%d" % k], 1)
+
+    for n, s in enumerate(sorted([2 * i, 2 * i + 1], key=late)):
+        stationary(s)
+        for k in range(K):
+            g.tensor.wait_ge(T.sem["qb%d" % k], 1)
+            product(k, s, T.bq, T.bsc, n == 0, False)
+    other = GR - 1 - i
     for k in range(K):
         g.tensor.wait_ge(T.sem["rem%d" % k], expect["rem%d" % k])
-        products(k, T.rq, T.rsc, GR - 1 - i, False, True)
+        for n, s in enumerate(sorted([2 * other, 2 * other + 1], key=late)):
+            stationary(s)
+            product(k, s, T.rq, T.rsc, False, n == 1)
 
     for k in range(K):
         lo, hi = START[k], START[k] + WIDTHS[k]

from concourse.bass import DstId, RemoteDMATransfer
from concourse.mybir import dt

GR, GC = 2, 4
NC = 512
AC = 128
WIDTHS = [128, 128, 128, 128]
K = len(WIDTHS)
START = [sum(WIDTHS[:k]) for k in range(K)]
HOSTS = 2

SCRATCH = {
    "abf": ("sbuf", [128, 4 * AC], "bfloat16"),
    "bbf": ("sbuf", [128, 2 * 4 * NC], "bfloat16"),
    "aq": ("sbuf", [128, GC * AC], "float8_e4m3fn_x4"),
    "asc": ("sbuf", [128, GC * AC], "uint8"),
    "bq": ("sbuf", [128, 2 * NC], "float8_e4m3fn_x4"),
    "bsc": ("sbuf", [128, 2 * NC], "uint8"),
    "rq": ("sbuf", [128, 2 * NC], "float8_e4m3fn_x4"),
    "rsc": ("sbuf", [128, 2 * NC], "uint8"),
    "ps": ("psum", [128, 512 * K], "float32"),
    "ysb": ("sbuf", [128, NC], "float32"),
}
CODES = ("aq", "bq", "rq")
NCALLS = 4 + 2 * K
SEMAPHORES = (["lda", "qa", "sent", "stored"] + ["a%d" % s for s in range(GC)]
              + ["ldb%d" % k for k in range(K)] + ["qb%d" % k for k in range(K)] + ["rem%d" % k for k in range(K)]
              + ["mm%d" % k for k in range(K)] + ["ev%d" % k for k in range(K)] + ["in%d" % c for c in range(NCALLS)])


def engines(mask):
    return [e for e in range(mask.bit_length()) if (mask >> e) & 1]


def as_mask(es):
    return sum(1 << e for e in es)


def view(T, name, lo, hi):
    ap = T[name][:, lo:hi]
    return ap.bitcast(dt.uint8) if name in CODES else ap


def block(k, m=0):
    return 2 * START[k] + m * WIDTHS[k]


def plan(rk, T, topo):
    r = T.rank_of(rk)
    i, j = r // GC, r % GC
    partner = T.cores[(GR - 1 - i) * GC + j]
    on = [T.cores[i * GC + (j + o) % GC] for o in range(1, GC)]
    chip = [c for c in range(HOSTS * topo.CORES_PER_HOST)
            if c != rk and topo.host(c) == topo.host(rk) and topo.chip(c) == topo.chip(rk)]
    porters = [c for c in chip if all(topo.may_write(c, d) for d in [partner] + on)]
    near = [c for c in porters if topo.die(c) == topo.die(rk)]
    far = [c for c in porters if topo.die(c) != topo.die(rk)]
    barred = [d for d in on if not topo.may_write(rk, d)]
    free = [d for d in on if topo.may_write(rk, d)]
    if j % 2:
        barred = barred[::-1]
    lo, hi, sem = AC * j, AC * j + AC, "a%d" % j
    calls = [
        ("qa", [("asc", "asc", lo, hi, "all", [(far[0], barred[0], sem), (near[0], barred[1], sem)])]),
        ("qa", [("aq", "aq", lo, hi, "all", [(near[1], barred[0], sem), (far[1], barred[1], sem)])]),
        ("qa", [("aq", "aq", lo, hi, "all", [(None, free[0], sem)])]),
        ("qa", [("asc", "asc", lo, hi, "all", [(None, free[0], sem)])]),
    ]
    for k in range(K):
        w = WIDTHS[k]
        calls.append(("qb%d" % k, [
            ("bq", "rq", block(k, 0), block(k, 0) + w, "even", [(near[k % 2], partner, "rem%d" % k)]),
            ("bq", "rq", block(k, 1), block(k, 1) + w, "odd", [(far[k % 2], partner, "rem%d" % k)])]))
        calls.append(("qb%d" % k, [
            ("bsc", "rsc", block(k), block(k) + 2 * w, "all", [((near, far)[k % 2][(k + 1) % 2], partner, "rem%d" % k)])]))
    return calls


def first_seen(xs):
    return [x for n, x in enumerate(xs) if x not in xs[:n]]


def share(mask, which):
    es = engines(mask)
    return es if which == "all" else es[0::2] if which == "even" else es[1::2]


def porter_program(g, core, rk, T, topo):
    sent = 0
    for c, (_, transfers) in enumerate(plan(rk, T, topo)):
        for (_, land, lo, hi, which, hops) in transfers:
            for (porter, dest, sem) in hops:
                if porter != core:
                    continue
                g.wait_ge(T.sem["in%d" % c], len(share(topo.mask(rk, core), which)))
                rid, pid = topo.addr(dest, core)
                mask = topo.mask(core, dest)
                g.remote_dma(view(T, land, lo, hi), view(T, land, lo, hi), T.sem[sem], T.sem.sent, pid, rid, mask)
                sent += len(engines(mask))
    if sent:
        g.wait_ge(T.sem.sent, sent)


def rank_program(g, core, T, topo):
    rank = T.rank_of(core)
    if rank is None:
        for rk in T.cores:
            if topo.host(rk) == topo.host(core) and topo.chip(rk) == topo.chip(core):
                porter_program(g, core, rk, T, topo)
        return
    i, j = rank // GC, rank % GC

    expect = {}
    for rk in T.cores:
        for (_, transfers) in plan(rk, T, topo):
            for (_, _, _, _, which, hops) in transfers:
                for (porter, dest, sem) in hops:
                    if dest == core:
                        n = len(share(topo.mask(rk, dest), which)) if porter is None else len(engines(topo.mask(porter, dest)))
                        expect[sem] = expect.get(sem, 0) + n

    g.sync.dma_start(T.abf[0:64, :], T.a[0:64, :]).then_inc(T.sem.lda, 16)
    g.scalar.dma_start(T.abf[64:128, :], T.a[64:128, :]).then_inc(T.sem.lda, 16)
    for k in range(K):
        for m, q in ((0, g.sync), (1, g.scalar)):
            q.dma_start(T.bbf[:, 4 * block(k, m):4 * (block(k, m) + WIDTHS[k])],
                        T.b[:, 4 * (NC * m + START[k]):4 * (NC * m + START[k] + WIDTHS[k])]).then_inc(T.sem["ldb%d" % k], 16)

    g.vector.wait_ge(T.sem.lda, 32)
    g.vector.quantize_mx(T.aq[:, AC * j:AC * j + AC], T.asc[:, AC * j:AC * j + AC], T.abf[:]).then_inc(T.sem.qa, 1)
    for k in range(K):
        lo, hi = block(k), block(k) + 2 * WIDTHS[k]
        g.vector.wait_ge(T.sem["ldb%d" % k], 32)
        g.vector.quantize_mx(T.bq[:, lo:hi], T.bsc[:, lo:hi], T.bbf[:, 4 * lo:4 * hi]).then_inc(T.sem["qb%d" % k], 1)

    sent = 0
    for c, (ready, transfers) in enumerate(plan(core, T, topo)):
        g.wait_ge(T.sem[ready], 1)
        ts = []
        for (src, land, lo, hi, which, hops) in transfers:
            if hops[0][0] is None:
                targets, landed = [hops[0][1]], T.sem[hops[0][2]]
            else:
                targets, landed = first_seen([h[0] for h in hops]), T.sem["in%d" % c]
            es = share(topo.mask(core, targets[0]), which)
            ids = [topo.addr(d, core) for d in targets]
            ts.append(RemoteDMATransfer(dst_ids=[DstId(rid=rid, pnc=pid) for (rid, pid) in ids],
                                        dma_engine_mask=as_mask(es), remote_sem=landed,
                                        srcs=[view(T, src, lo, hi)], dsts=[view(T, land, lo, hi) for _ in ids]))
            sent += len(es)
        g.remote_dma_fused(ts, local_sem=T.sem.sent)

    def late(s):
        return 0 if s == j else 1 if topo.may_write(T.cores[i * GC + s], core) else 2

    def stationary(s):
        if s == j:
            g.tensor.wait_ge(T.sem.qa, 1)
        else:
            g.tensor.wait_ge(T.sem["a%d" % s], expect["a%d" % s])

    def product(k, s, q, sc, start, stop):
        w, m = WIDTHS[k], s % 2
        g.tensor.matmul_mx(T.ps[:, 512 * k:512 * k + w], T.aq[:, AC * s:AC * s + AC], T.asc[:, AC * s:AC * s + AC],
                           q[:, block(k, m):block(k, m) + w], sc[:, block(k, m):block(k, m) + w],
                           start, stop).then_inc(T.sem["mm%d" % k], 1)

    for n, s in enumerate(sorted([2 * i, 2 * i + 1], key=late)):
        stationary(s)
        for k in range(K):
            g.tensor.wait_ge(T.sem["qb%d" % k], 1)
            product(k, s, T.bq, T.bsc, n == 0, False)
    other = GR - 1 - i
    for k in range(K):
        g.tensor.wait_ge(T.sem["rem%d" % k], expect["rem%d" % k])
        for n, s in enumerate(sorted([2 * other, 2 * other + 1], key=late)):
            stationary(s)
            product(k, s, T.rq, T.rsc, False, n == 1)

    for k in range(K):
        lo, hi = START[k], START[k] + WIDTHS[k]
        g.vector.wait_ge(T.sem["mm%d" % k], 2 * GR)
        g.vector.tensor_copy(T.ysb[:, lo:hi], T.ps[:, 512 * k:512 * k + WIDTHS[k]]).then_inc(T.sem["ev%d" % k], 1)
        g.sync.wait_ge(T.sem["ev%d" % k], 1)
        g.sync.dma_start(T.y[:, lo:hi], T.ysb[:, lo:hi]).then_inc(T.sem.stored, 16)
    g.sync.wait_ge(T.sem.stored, 16 * K)
    g.wait_ge(T.sem.sent, sent)
